import numpy as np
import ml_dtypes


def mxq(x, axis, fmt="e4m3"):
    dtype, down = {"e4m3": (ml_dtypes.float8_e4m3fn, 7), "e5m2": (ml_dtypes.float8_e5m2, 14)}[fmt]
    v = np.moveaxis(np.asarray(x, np.float32).astype(ml_dtypes.bfloat16).astype(np.float64), axis, -1)
    blocks = v.reshape(v.shape[:-1] + (-1, 32))
    amax = np.abs(blocks).max(-1, keepdims=True)
    byte = np.maximum(np.where(amax > 0, np.frexp(amax)[1] - 1 + 127, 0) - down, 1)
    scale = np.exp2(byte - 127.0)
    codes = (blocks / scale).astype(np.float32).astype(dtype).astype(np.float64)
    return np.moveaxis((codes * scale).reshape(v.shape), -1, axis)


WIDE = False


def mx_kscale(k):
    if not WIDE:
        return np.ones(k)
    levels = np.array([10, -10, 5, -5, 0])
    if k % 512:
        return np.exp2(np.random.permutation(np.resize(levels, k // 32))).repeat(32)
    a = np.empty((k // 512, 16))
    for p in range(k // 512):
        a[p, :8] = np.random.permutation(np.resize(levels, 8))
        for g in range(8):
            far = levels[np.abs(levels - a[p, g]) >= 10]
            a[p, g + 8] = far[np.random.randint(len(far))]
    return np.exp2(a.ravel()).repeat(32)


def f64(x):
    return np.asarray(x).astype(np.float64)


def striped(idx):
    return np.tile(idx.reshape(-1, 16).T, (8, 1)).astype(np.uint16)


def unstriped(offs):
    return offs[:16].T.reshape(-1).astype(np.int64)


E2M1 = np.array([0.0, 0.5, 1.0, 1.5, 2.0, 3.0, 4.0, 6.0, -0.0, -0.5, -1.0, -1.5, -2.0, -3.0, -4.0, -6.0])


def pack_weight(w, fmt):
    k, n = w.shape
    w = f64(np.asarray(w, np.float32).astype(ml_dtypes.bfloat16)).reshape(k // 32, 32, n)
    amax = np.abs(w).max(1)
    if fmt == "e4m3":
        byte = np.frexp(amax)[1] - 1 + 127 - 7
    else:
        mant, ex = np.frexp(amax / 6.0)
        byte = np.where(mant > 0.5, ex, ex - 1) + 127
    byte = np.clip(np.where(amax > 0, byte, 1), 1, 254)
    scaled = (w * np.exp2(127.0 - byte)[:, None, :]).reshape(k, n).astype(np.float32)
    by_word = np.ascontiguousarray(scaled.reshape(k // 512, 128, 4, n).transpose(0, 1, 3, 2))
    if fmt == "e4m3":
        words = by_word.astype(ml_dtypes.float8_e4m3fn).view(np.uint8)
    else:
        c = by_word.astype(ml_dtypes.float4_e2m1fn).view(np.uint8) & 0xF
        words = (c[..., 0::2] | (c[..., 1::2] << 4)).reshape(k // 512, 128, 2 * n)
    return np.ascontiguousarray(words), np.ascontiguousarray(byte.astype(np.uint8).reshape(k // 512, 16, n))


def unpack_weight(words, scales, fmt):
    g, _, n = scales.shape
    words = np.ascontiguousarray(words).reshape(g, 128, n, -1)
    if fmt == "e4m3":
        vals = words.view(ml_dtypes.float8_e4m3fn).astype(np.float64)
    else:
        nib = np.empty((g, 128, n, 4), np.uint8)
        nib[..., 0::2] = words & 0xF
        nib[..., 1::2] = words >> 4
        vals = E2M1[nib]
    vals = vals * np.repeat(np.exp2(scales.astype(np.float64) - 127.0), 8, axis=1)[..., None]
    return vals.transpose(0, 1, 3, 2).reshape(g * 512, n)


def gelu(v):
    return 0.5 * v * (1.0 + np.tanh(np.sqrt(2.0 / np.pi) * (v + 0.044715 * v**3)))


K, H, N, T, S, P1, P2, P3 = 512, 1024, 512, 4096, 2048, 1024, 512, 256

def setup_inputs():
    n = np.random.standard_normal
    s = mx_kscale(K)[:, None]
    u = mx_kscale(H)[:, None]
    tab_words, tab_scales = pack_weight(n((K, T)) * s, "e4m3")
    w1 = n((K, H)) / np.sqrt(K) / s * u.T
    w4_words, w4_scales = pack_weight(n((K, H)) / np.sqrt(K) / s * u.T, "e2m1")
    w3 = 0.9 * n((H, N)) / np.sqrt(H) / u**2
    w8_words, w8_scales = pack_weight(0.4 * n((H, N)) / np.sqrt(H) / u**2, "e4m3")
    return {"tab_words": tab_words, "tab_scales": tab_scales,
            "offs": striped(np.random.permutation(T)[:S]),
            "pos1": striped(np.random.permutation(S)[:P1]),
            "pos2": striped(np.random.permutation(S)[:P1]),
            "pos3": striped(np.random.permutation(P1)[:P2]),
            "pos4": striped(np.random.permutation(P1)[:P2]),
            "pos5": striped(np.random.permutation(P2)[:P3]),
            "pos6": striped(np.random.permutation(P2)[:P3]),
            "w1": w1.astype(np.float32),
            "w4_words": w4_words, "w4_scales": w4_scales,
            "w3": w3.astype(np.float32),
            "w8_words": w8_words, "w8_scales": w8_scales}

def reference(tab_words, tab_scales, offs, pos1, pos2, pos3, pos4, pos5, pos6,
              w1, w4_words, w4_scales, w3, w8_words, w8_scales):
    v = unpack_weight(tab_words, tab_scales, "e4m3")[:, unstriped(offs)]
    ha = mxq(f64(w1), 0, "e4m3").T @ v
    hb = unpack_weight(w4_words, w4_scales, "e2m1").T @ v
    h = np.maximum(ha, hb)
    a1 = h[:, unstriped(pos1)] - h[:, unstriped(pos2)]
    a2 = a1[:, unstriped(pos3)] * a1[:, unstriped(pos4)]
    a3 = np.minimum(a2[:, unstriped(pos5)], a2[:, unstriped(pos6)])
    xq = mxq(a3, 0, "e4m3")
    ya = mxq(f64(w3), 0, "e4m3").T @ xq
    yb = unpack_weight(w8_words, w8_scales, "e4m3").T @ xq
    return np.tanh(ya) * np.cos(yb)

@@ -1,0 +1,279 @@
+from contextlib import ExitStack
+
+import concourse.mybir as mybir
+
+K, H, N, T, S, P1, P2, P3 = 512, 1024, 512, 4096, 2048, 1024, 512, 256
+FLOPS = 2 * 2 * K * H * S + 2 * 2 * H * N * P3
+
+F32 = mybir.dt.float32
+BF16 = mybir.dt.bfloat16
+I32 = mybir.dt.int32
+U32 = mybir.dt.uint32
+U16 = mybir.dt.uint16
+U8 = mybir.dt.uint8
+FP8X4 = mybir.dt.float8_e4m3fn_x4
+FP4X4 = mybir.dt.float4_e2m1fn_x4
+ALU = mybir.AluOpType
+ACT = mybir.ActivationFunctionType
+
+P = 128
+PACK = 4
+PASS = P * PACK
+GROUPS = H // PASS
+SLICES = GROUPS * PACK
+CHUNK = 512
+CHUNKS = S // CHUNK
+QUADS = 4
+LIST_ROWS = 16
+
+
+def tile_list_pitch_jury_scores_kernel(
+    tc, tab_words, tab_scales, offs, pos1, pos2, pos3, pos4, pos5, pos6,
+    w1, w4_words, w4_scales, w3, w8_words, w8_scales, out,
+):
+    nc = tc.nc
+    with ExitStack() as ctx:
+        keep = ctx.enter_context(tc.tile_pool(name="keep", bufs=1))
+        ring = ctx.enter_context(tc.tile_pool(name="ring", bufs=2))
+        psum = ctx.enter_context(tc.psum_pool(name="psum", bufs=4))
+
+        def load_list(src, name):
+            tile = keep.tile([P, src.shape[1]], U16, name=name)
+            nc.sync.dma_start(tile[:], src)
+            return tile
+
+        tab_plane = keep.tile([P, T], U8, align_bytes=64)
+        w4_plane_raw = keep.tile([P, H], U8, align_bytes=64)
+        w8_plane = keep.tile([P, GROUPS, N], U8, align_bytes=64)
+        nc.vector.memset(tab_plane[:].bitcast(I32), 0)
+        nc.vector.memset(w4_plane_raw[:].bitcast(I32), 0)
+        nc.vector.memset(w8_plane[:].rearrange("p a n -> p (a n)").bitcast(I32), 0)
+
+        offs_sb = load_list(offs, "offs_sb")
+        for q in range(QUADS):
+            nc.scalar.dma_start(
+                tab_plane[32 * q : 32 * q + 4, :].bitcast(I32), tab_scales[0, 4 * q : 4 * q + 4, :].bitcast(I32)
+            )
+        w4_raw = keep.tile([P, 2 * H], U8, align_bytes=64)
+        nc.sync.dma_start(w4_raw[:].bitcast(I32), w4_words[0].bitcast(I32))
+
+        def load_rows(src):
+            raw = ring.tile([P, PACK, PASS], F32, name="raw")
+            nc.sync.dma_start(raw[:], src.rearrange("(p j) c -> p j c", j=PACK))
+            return raw
+
+        w1_raw = [load_rows(w1[:, 0:PASS])]
+        tab_sb = keep.tile([P, T], I32, align_bytes=64)
+        nc.sync.dma_start(tab_sb[:], tab_words[0].rearrange("p t i -> p (t i)").bitcast(I32))
+        for q in range(QUADS):
+            nc.sync.dma_start(
+                w4_plane_raw[32 * q : 32 * q + 4, :].bitcast(I32), w4_scales[0, 4 * q : 4 * q + 4, :].bitcast(I32)
+            )
+        p1_sb = load_list(pos1, "p1_sb")
+        p2_sb = load_list(pos2, "p2_sb")
+        w1_raw.append(load_rows(w1[:, PASS : 2 * PASS]))
+        p3_sb = load_list(pos3, "p3_sb")
+        p4_sb = load_list(pos4, "p4_sb")
+        p5_sb = load_list(pos5, "p5_sb")
+        p6_sb = load_list(pos6, "p6_sb")
+        w8_codes = keep.tile([P, GROUPS, N], I32, align_bytes=64)
+        nc.sync.dma_start(w8_codes[:], w8_words.rearrange("a p n i -> p a (n i)").bitcast(I32))
+        for r in range(4):
+            nc.sync.dma_start(
+                w8_plane[r:P:32, :, :].bitcast(I32),
+                w8_scales.rearrange("a (q r) n -> r q a n", r=4)[r].bitcast(I32),
+            )
+
+        w4_codes = [keep.tile([P, 2 * PASS], U8, align_bytes=64, name="w4_codes%d" % g) for g in range(GROUPS)]
+        w4_plane = [keep.tile([P, PASS], U8, align_bytes=64, name="w4_plane%d" % g) for g in range(GROUPS)]
+        w1_codes = [keep.tile([P, PASS], U32, align_bytes=64, name="w1_codes%d" % g) for g in range(GROUPS)]
+        w1_plane = [keep.tile([P, PASS], U8, align_bytes=64, name="w1_plane%d" % g) for g in range(GROUPS)]
+        w3_codes = [keep.tile([P, N], U32, align_bytes=64, name="w3_codes%d" % g) for g in range(GROUPS)]
+        w3_plane = [keep.tile([P, N], U8, align_bytes=64, name="w3_plane%d" % g) for g in range(GROUPS)]
+        x_codes = [keep.tile([P, P3], U32, align_bytes=64, name="x_codes%d" % g) for g in range(GROUPS)]
+        x_plane = [keep.tile([P, P3], U8, align_bytes=64, name="x_plane%d" % g) for g in range(GROUPS)]
+        v_codes = [keep.tile([P, CHUNK], U32, align_bytes=64, name="v_codes%d" % c) for c in range(CHUNKS)]
+        v_plane = keep.tile([P, S], U8, align_bytes=64)
+
+        def deal_w4_words(g):
+            nc.vector.tensor_copy(
+                w4_codes[g][:].rearrange("p (t m b) -> p t m b", t=PACK, b=2),
+                w4_raw[:, 2 * PASS * g : 2 * PASS * (g + 1)].rearrange("p (m t b) -> p t m b", t=PACK, b=2),
+            )
+
+        def deal_w4_plane(g):
+            nc.vector.tensor_copy(
+                w4_plane[g][:].rearrange("p (t m) -> p t m", t=PACK),
+                w4_plane_raw[:, PASS * g : PASS * (g + 1)].rearrange("p (m t) -> p t m", t=PACK),
+            )
+
+        def round_w1(g):
+            grouped = ring.tile([P, PASS * PACK], BF16, align_bytes=64, name="grouped")
+            nc.scalar.copy(
+                grouped[:].rearrange("p (t m j) -> p m j t", t=PACK, j=PACK),
+                w1_raw[g][:].rearrange("p j (m t) -> p m j t", t=PACK),
+            )
+            return grouped
+
+        def round_w3(raw):
+            grouped = ring.tile([P, N * PACK], BF16, align_bytes=64, name="grouped")
+            nc.scalar.copy(
+                grouped[:].rearrange("p (c i j) -> p c j i", i=4, j=PACK),
+                raw[:].rearrange("p j (c i) -> p c j i", i=4),
+            )
+            return grouped
+
+        def quantize(codes, plane, grouped):
+            nc.vector.quantize_mx(out=codes[:].bitcast(FP8X4), scales=plane[:], in_=grouped[:])
+
+        ha_sb = {}
+        hb_ps = {}
+        h_sb = {}
+
+        def products(s, c):
+            g, t = divmod(s, PACK)
+            cols = slice(CHUNK * c, CHUNK * (c + 1))
+            if c == 0:
+                ha_sb[s] = ring.tile([P, S], F32, name="ha_sb")
+            ha_ps = psum.tile([P, CHUNK], F32, name="bank_a")
+            nc.tensor.matmul_mx(
+                out=ha_ps[:],
+                lhsT=w1_codes[g][:, P * t : P * (t + 1)].bitcast(FP8X4),
+                lhsT_scale=w1_plane[g][:, P * t : P * (t + 1)],
+                rhs=v_codes[c][:].bitcast(FP8X4),
+                rhs_scale=v_plane[:, cols],
+                start=True, stop=True,
+            )
+            hb_ps[s, c] = psum.tile([P, CHUNK], F32, name="bank_b")
+            nc.tensor.matmul_mx(
+                out=hb_ps[s, c][:],
+                lhsT=w4_codes[g][:, 2 * P * t : 2 * P * (t + 1)].bitcast(FP4X4),
+                lhsT_scale=w4_plane[g][:, P * t : P * (t + 1)],
+                rhs=v_codes[c][:].bitcast(FP8X4),
+                rhs_scale=v_plane[:, cols],
+                start=True, stop=True,
+            )
+            nc.scalar.copy(ha_sb[s][:, cols], ha_ps[:])
+
+        def larger(s, c):
+            if s >= SLICES:
+                return
+            cols = slice(CHUNK * c, CHUNK * (c + 1))
+            if c == 0:
+                h_sb[s] = ring.tile([P, S], F32, name="h_sb")
+            nc.vector.tensor_tensor(h_sb[s][:, cols], hb_ps[s, c][:], ha_sb[s][:, cols], ALU.max)
+
+        deal_w4_words(0)
+        nc.vector.tensor_copy(v_plane[:], tab_plane[:].indirect(offs_sb[:]))
+        deal_w4_plane(0)
+        quantize(w1_codes[0], w1_plane[0], round_w1(0))
+        per_chunk = CHUNK // LIST_ROWS
+        for c in range(CHUNKS):
+            nc.vector.tensor_copy(
+                v_codes[c][:], tab_sb[:].bitcast(U32).indirect(offs_sb[:, per_chunk * c : per_chunk * (c + 1)])
+            )
+            products(0, c)
+            if c > 0:
+                larger(0, c - 1)
+        w1_grouped = round_w1(1)
+        deal_w4_words(1)
+        larger(0, CHUNKS - 1)
+        for c in range(CHUNKS):
+            products(1, c)
+        deal_w4_plane(1)
+        quantize(w1_codes[1], w1_plane[1], w1_grouped)
+        w3_raw = [load_rows(w3[PASS * g : PASS * (g + 1), :]) for g in range(GROUPS)]
+
+        a3_sb = [keep.tile([P, PACK, P3], BF16, name="a3_sb%d" % g) for g in range(GROUPS)]
+        pairs = {}
+
+        def smaller(s):
+            g, t = divmod(s, PACK)
+            nc.vector.tensor_tensor(a3_sb[g][:, t, :], pairs[s][0][:], pairs[s][1][:], ALU.min)
+
+        def weave(engine_copy, g):
+            woven = ring.tile([P, P3 * PACK], BF16, align_bytes=64, name="woven")
+            engine_copy(
+                woven[:].rearrange("p (c i t) -> p c t i", i=4, t=PACK),
+                a3_sb[g][:].rearrange("p t (c i) -> p c t i", i=4),
+            )
+            return woven
+
+        def refill(s, c):
+            if s < SLICES:
+                products(s, c)
+
+        w3_grouped = {}
+        woven0 = None
+        for s in range(SLICES):
+            h = h_sb[s]
+            g2 = ring.tile([P, P1], F32, name="g2")
+            nc.vector.tensor_copy(g2[:], h[:].indirect(p2_sb[:]))
+            if s > 0:
+                smaller(s - 1)
+            if s == PACK:
+                woven0 = weave(nc.scalar.copy, 0)
+            larger(s + 1, 0)
+            refill(s + 2, 0)
+            a1 = ring.tile([P, P1], F32, name="a1")
+            nc.vector.tensor_tensor(a1[:], h[:].indirect(p1_sb[:]), g2[:], ALU.subtract)
+            larger(s + 1, 1)
+            refill(s + 2, 1)
+            g4 = ring.tile([P, P2], F32, name="g4")
+            nc.vector.tensor_copy(g4[:], a1[:].indirect(p4_sb[:]))
+            larger(s + 1, 2)
+            refill(s + 2, 2)
+            a2 = ring.tile([P, P2], F32, name="a2")
+            nc.vector.tensor_tensor(a2[:], a1[:].indirect(p3_sb[:]), g4[:], ALU.mult)
+            larger(s + 1, 3)
+            refill(s + 2, 3)
+            g5 = ring.tile([P, P3], F32, name="g5")
+            g6 = ring.tile([P, P3], F32, name="g6")
+            nc.vector.tensor_copy(g5[:], a2[:].indirect(p5_sb[:]))
+            nc.vector.tensor_copy(g6[:], a2[:].indirect(p6_sb[:]))
+            pairs[s] = (g5, g6)
+            if s in (1, 2):
+                w3_grouped[s - 1] = round_w3(w3_raw[s - 1])
+            if s in (2, 3):
+                quantize(w3_codes[s - 2], w3_plane[s - 2], w3_grouped[s - 2])
+            if s == PACK:
+                quantize(x_codes[0], x_plane[0], woven0)
+
+        y_ps = [psum.tile([P, 2, P3], F32, name="bank_a") for b in range(4)]
+
+        def second_stage(g):
+            for b in range(4):
+                for half in range(2):
+                    nb = 2 * (b % 2) + half
+                    cols = slice(P * nb, P * (nb + 1))
+                    if b < 2:
+                        codes, plane = w3_codes[g][:, cols], w3_plane[g][:, cols]
+                    else:
+                        codes, plane = w8_codes[:, g, cols], w8_plane[:, g, cols]
+                    nc.tensor.matmul_mx(
+                        out=y_ps[b][:, half, :],
+                        lhsT=codes.bitcast(FP8X4),
+                        lhsT_scale=plane,
+                        rhs=x_codes[g][:].bitcast(FP8X4),
+                        rhs_scale=x_plane[g][:],
+                        start=(g == 0 and half == 0),
+                        stop=(g == GROUPS - 1 and half == 1),
+                    )
+
+        second_stage(0)
+        smaller(SLICES - 1)
+        quantize(x_codes[1], x_plane[1], weave(nc.vector.tensor_copy, 1))
+        second_stage(1)
+
+        tanh_sb = [keep.tile([P, 2, P3], F32, name="tanh_sb%d" % b) for b in range(2)]
+        sin_sb = [keep.tile([P, 2, P3], F32, name="sin_sb%d" % b) for b in range(2)]
+        for b in range(2):
+            nc.scalar.activation(tanh_sb[b][:], y_ps[b][:], ACT.Tanh)
+        for b in range(2):
+            nc.scalar.activation(sin_sb[b][:], y_ps[2 + b][:], ACT.Sin, scale=0.5)
+        for b in range(2):
+            sq = ring.tile([P, 2, P3], F32, name="sq")
+            nc.vector.scalar_tensor_tensor(sq[:], sin_sb[b][:], -2.0, sin_sb[b][:], ALU.mult, ALU.mult)
+            res = ring.tile([P, 2, P3], F32, name="res")
+            nc.vector.scalar_tensor_tensor(res[:], sq[:], 1.0, tanh_sb[b][:], ALU.add, ALU.mult)
+            nc.sync.dma_start(out[2 * P * b : 2 * P * (b + 1), :].rearrange("(h p) j -> p h j", p=P), res[:])

@@ -25,6 +25,8 @@ CHUNK = 512
 CHUNKS = S // CHUNK
 QUADS = 4
 LIST_ROWS = 16
+OFFLOAD = [0, 1, 2, 2, 2, 2, 2, 2]
+G_WIDTH = 512
 
 
 def tile_list_pitch_jury_scores_kernel(
@@ -35,6 +37,7 @@ def tile_list_pitch_jury_scores_kernel(
     with ExitStack() as ctx:
         keep = ctx.enter_context(tc.tile_pool(name="keep", bufs=1))
         ring = ctx.enter_context(tc.tile_pool(name="ring", bufs=2))
+        ring3 = ctx.enter_context(tc.tile_pool(name="ring3", bufs=3))
         psum = ctx.enter_context(tc.psum_pool(name="psum", bufs=4))
 
         def load_list(src, name):
@@ -45,30 +48,29 @@ def tile_list_pitch_jury_scores_kernel(
         tab_plane = keep.tile([P, T], U8, align_bytes=64)
         w4_plane_raw = keep.tile([P, H], U8, align_bytes=64)
         w8_plane = keep.tile([P, GROUPS, N], U8, align_bytes=64)
-        nc.vector.memset(tab_plane[:].bitcast(I32), 0)
-        nc.vector.memset(w4_plane_raw[:].bitcast(I32), 0)
-        nc.vector.memset(w8_plane[:].rearrange("p a n -> p (a n)").bitcast(I32), 0)
+        nc.gpsimd.memset(w8_plane[:].rearrange("p a n -> p (a n)").bitcast(I32), 0)
 
-        offs_sb = load_list(offs, "offs_sb")
-        for q in range(QUADS):
-            nc.scalar.dma_start(
-                tab_plane[32 * q : 32 * q + 4, :].bitcast(I32), tab_scales[0, 4 * q : 4 * q + 4, :].bitcast(I32)
-            )
-        w4_raw = keep.tile([P, 2 * H], U8, align_bytes=64)
-        nc.sync.dma_start(w4_raw[:].bitcast(I32), w4_words[0].bitcast(I32))
+        def load_plane(plane, scales):
+            for q in range(QUADS):
+                rows = scales[0, 4 * q : 4 * q + 4, :].bitcast(I32)
+                nc.sync.dma_start(
+                    plane[32 * q : 32 * (q + 1), :].bitcast(I32),
+                    rows.unsqueeze(0).broadcast_to([8, 4, rows.shape[1]]),
+                )
 
         def load_rows(src):
             raw = ring.tile([P, PACK, PASS], F32, name="raw")
             nc.sync.dma_start(raw[:], src.rearrange("(p j) c -> p j c", j=PACK))
             return raw
 
-        w1_raw = [load_rows(w1[:, 0:PASS])]
+        offs_sb = load_list(offs, "offs_sb")
+        load_plane(tab_plane, tab_scales)
+        w4_raw = keep.tile([P, 2 * H], U8, align_bytes=64)
+        nc.sync.dma_start(w4_raw[:].bitcast(I32), w4_words[0].bitcast(I32))
         tab_sb = keep.tile([P, T], I32, align_bytes=64)
         nc.sync.dma_start(tab_sb[:], tab_words[0].rearrange("p t i -> p (t i)").bitcast(I32))
-        for q in range(QUADS):
-            nc.sync.dma_start(
-                w4_plane_raw[32 * q : 32 * q + 4, :].bitcast(I32), w4_scales[0, 4 * q : 4 * q + 4, :].bitcast(I32)
-            )
+        load_plane(w4_plane_raw, w4_scales)
+        w1_raw = [load_rows(w1[:, 0:PASS])]
         p1_sb = load_list(pos1, "p1_sb")
         p2_sb = load_list(pos2, "p2_sb")
         w1_raw.append(load_rows(w1[:, PASS : 2 * PASS]))
@@ -92,17 +94,17 @@ def tile_list_pitch_jury_scores_kernel(
         w3_plane = [keep.tile([P, N], U8, align_bytes=64, name="w3_plane%d" % g) for g in range(GROUPS)]
         x_codes = [keep.tile([P, P3], U32, align_bytes=64, name="x_codes%d" % g) for g in range(GROUPS)]
         x_plane = [keep.tile([P, P3], U8, align_bytes=64, name="x_plane%d" % g) for g in range(GROUPS)]
-        v_codes = [keep.tile([P, CHUNK], U32, align_bytes=64, name="v_codes%d" % c) for c in range(CHUNKS)]
+        v_codes = {}
         v_plane = keep.tile([P, S], U8, align_bytes=64)
 
         def deal_w4_words(g):
-            nc.vector.tensor_copy(
+            nc.gpsimd.tensor_copy(
                 w4_codes[g][:].rearrange("p (t m b) -> p t m b", t=PACK, b=2),
                 w4_raw[:, 2 * PASS * g : 2 * PASS * (g + 1)].rearrange("p (m t b) -> p t m b", t=PACK, b=2),
             )
 
         def deal_w4_plane(g):
-            nc.vector.tensor_copy(
+            nc.gpsimd.tensor_copy(
                 w4_plane[g][:].rearrange("p (t m) -> p t m", t=PACK),
                 w4_plane_raw[:, PASS * g : PASS * (g + 1)].rearrange("p (m t) -> p t m", t=PACK),
             )
@@ -124,17 +126,35 @@ def tile_list_pitch_jury_scores_kernel(
             return grouped
 
         def quantize(codes, plane, grouped):
-            nc.vector.quantize_mx(out=codes[:].bitcast(FP8X4), scales=plane[:], in_=grouped[:])
+            nc.vector.quantize_mx(out=codes.bitcast(FP8X4), scales=plane, in_=grouped)
 
         ha_sb = {}
         hb_ps = {}
         h_sb = {}
 
+        def product_b(s, c):
+            g, t = divmod(s, PACK)
+            hb_ps[s, c] = psum.tile([P, CHUNK], F32, name="bank_b")
+            nc.tensor.matmul_mx(
+                out=hb_ps[s, c][:],
+                lhsT=w4_codes[g][:, 2 * P * t : 2 * P * (t + 1)].bitcast(FP4X4),
+                lhsT_scale=w4_plane[g][:, P * t : P * (t + 1)],
+                rhs=v_codes[c][:].bitcast(FP8X4),
+                rhs_scale=v_plane[:, CHUNK * c : CHUNK * (c + 1)],
+                start=True, stop=True,
+            )
+
         def products(s, c):
+            if s < SLICES:
+                product_b(s, c)
+                product_a(s, c)
+
+        def product_a(s, c):
             g, t = divmod(s, PACK)
             cols = slice(CHUNK * c, CHUNK * (c + 1))
             if c == 0:
-                ha_sb[s] = ring.tile([P, S], F32, name="ha_sb")
+                ha_sb[s] = ring3.tile([P, S], F32, name="ha_sb")
+                h_sb[s] = ring.tile([P, S], F32, name="h_sb")
             ha_ps = psum.tile([P, CHUNK], F32, name="bank_a")
             nc.tensor.matmul_mx(
                 out=ha_ps[:],
@@ -144,44 +164,57 @@ def tile_list_pitch_jury_scores_kernel(
                 rhs_scale=v_plane[:, cols],
                 start=True, stop=True,
             )
-            hb_ps[s, c] = psum.tile([P, CHUNK], F32, name="bank_b")
-            nc.tensor.matmul_mx(
-                out=hb_ps[s, c][:],
-                lhsT=w4_codes[g][:, 2 * P * t : 2 * P * (t + 1)].bitcast(FP4X4),
-                lhsT_scale=w4_plane[g][:, P * t : P * (t + 1)],
-                rhs=v_codes[c][:].bitcast(FP8X4),
-                rhs_scale=v_plane[:, cols],
-                start=True, stop=True,
-            )
             nc.scalar.copy(ha_sb[s][:, cols], ha_ps[:])
+            if c < OFFLOAD[s]:
+                hb_sb = ring.tile([P, CHUNK], F32, name="hb_sb")
+                nc.scalar.copy(hb_sb[:], hb_ps[s, c][:])
+                for u in range(CHUNK // G_WIDTH):
+                    part = slice(G_WIDTH * u, G_WIDTH * (u + 1))
+                    whole = slice(CHUNK * c + G_WIDTH * u, CHUNK * c + G_WIDTH * (u + 1))
+                    excess = ring3.tile([P, G_WIDTH], F32, name="excess")
+                    nc.gpsimd.tensor_tensor(excess[:], hb_sb[:, part], ha_sb[s][:, whole], ALU.subtract)
+                    kept = ring3.tile([P, G_WIDTH], F32, name="kept")
+                    nc.scalar.activation(kept[:], excess[:], ACT.Relu)
+                    nc.gpsimd.tensor_tensor(h_sb[s][:, whole], ha_sb[s][:, whole], kept[:], ALU.add)
 
         def larger(s, c):
-            if s >= SLICES:
+            if s >= SLICES or c < OFFLOAD[s]:
                 return
             cols = slice(CHUNK * c, CHUNK * (c + 1))
-            if c == 0:
-                h_sb[s] = ring.tile([P, S], F32, name="h_sb")
             nc.vector.tensor_tensor(h_sb[s][:, cols], hb_ps[s, c][:], ha_sb[s][:, cols], ALU.max)
 
         deal_w4_words(0)
         nc.vector.tensor_copy(v_plane[:], tab_plane[:].indirect(offs_sb[:]))
         deal_w4_plane(0)
-        quantize(w1_codes[0], w1_plane[0], round_w1(0))
+        first = keep.tile([P, P * PACK], BF16, align_bytes=64, name="v_codes%d" % (CHUNKS - 1))
+        rest = keep.tile([P, (PACK - 1) * P * PACK], BF16, align_bytes=64)
+        by_slot = w1_raw[0][:].rearrange("p j (m t) -> p m j t", t=PACK)
+        nc.scalar.copy(first[:].rearrange("p (m j) -> p m j", j=PACK), by_slot[:, :, :, 0])
+        nc.gpsimd.tensor_copy(
+            rest[:].rearrange("p (t m j) -> p t m j", t=PACK - 1, j=PACK),
+            w1_raw[0][:].rearrange("p j (m t) -> p t m j", t=PACK)[:, 1:PACK, :, :],
+        )
         per_chunk = CHUNK // LIST_ROWS
         for c in range(CHUNKS):
+            if c == CHUNKS - 1:
+                quantize(w1_codes[0][:, 0:P], w1_plane[0][:, 0:P], first[:])
+                for early in range(c):
+                    product_a(0, early)
+            v_codes[c] = keep.tile([P, CHUNK], U32, align_bytes=64, name="v_codes%d" % c)
             nc.vector.tensor_copy(
                 v_codes[c][:], tab_sb[:].bitcast(U32).indirect(offs_sb[:, per_chunk * c : per_chunk * (c + 1)])
             )
-            products(0, c)
-            if c > 0:
-                larger(0, c - 1)
-        w1_grouped = round_w1(1)
-        deal_w4_words(1)
+            product_b(0, c)
+        product_a(0, CHUNKS - 1)
+        for c in range(CHUNKS - 1):
+            larger(0, c)
+        quantize(w1_codes[0][:, P:PASS], w1_plane[0][:, P:PASS], rest[:])
         larger(0, CHUNKS - 1)
         for c in range(CHUNKS):
             products(1, c)
+        deal_w4_words(1)
         deal_w4_plane(1)
-        quantize(w1_codes[1], w1_plane[1], w1_grouped)
+        w1_grouped = round_w1(1)
         w3_raw = [load_rows(w3[PASS * g : PASS * (g + 1), :]) for g in range(GROUPS)]
 
         a3_sb = [keep.tile([P, PACK, P3], BF16, name="a3_sb%d" % g) for g in range(GROUPS)]
@@ -189,7 +222,7 @@ def tile_list_pitch_jury_scores_kernel(
 
         def smaller(s):
             g, t = divmod(s, PACK)
-            nc.vector.tensor_tensor(a3_sb[g][:, t, :], pairs[s][0][:], pairs[s][1][:], ALU.min)
+            nc.vector.tensor_tensor(a3_sb[g][:, t, :], pairs[s][0], pairs[s][1], ALU.min)
 
         def weave(engine_copy, g):
             woven = ring.tile([P, P3 * PACK], BF16, align_bytes=64, name="woven")
@@ -199,81 +232,88 @@ def tile_list_pitch_jury_scores_kernel(
             )
             return woven
 
-        def refill(s, c):
-            if s < SLICES:
-                products(s, c)
-
         w3_grouped = {}
+        a1_sb = {}
+        a2_sb = {}
         woven0 = None
-        for s in range(SLICES):
-            h = h_sb[s]
-            g2 = ring.tile([P, P1], F32, name="g2")
-            nc.vector.tensor_copy(g2[:], h[:].indirect(p2_sb[:]))
-            if s > 0:
-                smaller(s - 1)
-            if s == PACK:
+        for k in range(SLICES + 2):
+            level1, level2, level3 = k < SLICES, 1 <= k <= SLICES, k >= 2
+            spare = ha_sb[k] if level1 else ring3.tile([P, S], F32, name="ha_sb")
+            g4, g5, g6 = spare[:, 256:768], spare[:, 768:1024], spare[:, 0:256]
+            if level1:
+                g2 = ring.tile([P, P1], F32, name="g2")
+                nc.vector.tensor_copy(g2[:], h_sb[k][:].indirect(p2_sb[:]))
+            if level2:
+                nc.vector.tensor_copy(g4, a1_sb[k - 1][:].indirect(p4_sb[:]))
+            if level3:
+                nc.vector.tensor_copy(g5, a2_sb[k - 2][:].indirect(p5_sb[:]))
+            if level1:
+                a1_sb[k] = ring.tile([P, P1], F32, name="a1")
+                nc.vector.tensor_tensor(a1_sb[k][:], h_sb[k][:].indirect(p1_sb[:]), g2[:], ALU.subtract)
+            if level3:
+                nc.vector.tensor_copy(g6, a2_sb[k - 2][:].indirect(p6_sb[:]))
+            if level2:
+                a2_sb[k - 1] = ring.tile([P, P2], F32, name="a2")
+                nc.vector.tensor_tensor(a2_sb[k - 1][:], a1_sb[k - 1][:].indirect(p3_sb[:]), g4, ALU.mult)
+            if level3:
+                pairs[k - 2] = (g5, g6)
+                smaller(k - 2)
+            for c in range(CHUNKS):
+                larger(k + 1, c)
+                products(k + 2, c)
+            if k == 0:
+                quantize(w1_codes[1][:], w1_plane[1][:], w1_grouped[:])
+            if k in (1, 2):
+                w3_grouped[k - 1] = round_w3(w3_raw[k - 1])
+            if k in (2, 3):
+                quantize(w3_codes[k - 2][:], w3_plane[k - 2][:], w3_grouped[k - 2][:])
+            if k == PACK + 1:
                 woven0 = weave(nc.scalar.copy, 0)
-            larger(s + 1, 0)
-            refill(s + 2, 0)
-            a1 = ring.tile([P, P1], F32, name="a1")
-            nc.vector.tensor_tensor(a1[:], h[:].indirect(p1_sb[:]), g2[:], ALU.subtract)
-            larger(s + 1, 1)
-            refill(s + 2, 1)
-            g4 = ring.tile([P, P2], F32, name="g4")
-            nc.vector.tensor_copy(g4[:], a1[:].indirect(p4_sb[:]))
-            larger(s + 1, 2)
-            refill(s + 2, 2)
-            a2 = ring.tile([P, P2], F32, name="a2")
-            nc.vector.tensor_tensor(a2[:], a1[:].indirect(p3_sb[:]), g4[:], ALU.mult)
-            larger(s + 1, 3)
-            refill(s + 2, 3)
-            g5 = ring.tile([P, P3], F32, name="g5")
-            g6 = ring.tile([P, P3], F32, name="g6")
-            nc.vector.tensor_copy(g5[:], a2[:].indirect(p5_sb[:]))
-            nc.vector.tensor_copy(g6[:], a2[:].indirect(p6_sb[:]))
-            pairs[s] = (g5, g6)
-            if s in (1, 2):
-                w3_grouped[s - 1] = round_w3(w3_raw[s - 1])
-            if s in (2, 3):
-                quantize(w3_codes[s - 2], w3_plane[s - 2], w3_grouped[s - 2])
-            if s == PACK:
-                quantize(x_codes[0], x_plane[0], woven0)
+            if k == PACK + 2:
+                quantize(x_codes[0][:], x_plane[0][:], woven0[:])
 
-        y_ps = [psum.tile([P, 2, P3], F32, name="bank_a") for b in range(4)]
+        blocks = N // P
+        ya_ps = [psum.tile([P, P3], F32, name="bank_a") for nb in range(blocks)]
+        yb_ps = [psum.tile([P, P3], F32, name="bank_b") for nb in range(blocks)]
 
-        def second_stage(g):
-            for b in range(4):
-                for half in range(2):
-                    nb = 2 * (b % 2) + half
-                    cols = slice(P * nb, P * (nb + 1))
-                    if b < 2:
-                        codes, plane = w3_codes[g][:, cols], w3_plane[g][:, cols]
-                    else:
-                        codes, plane = w8_codes[:, g, cols], w8_plane[:, g, cols]
-                    nc.tensor.matmul_mx(
-                        out=y_ps[b][:, half, :],
-                        lhsT=codes.bitcast(FP8X4),
-                        lhsT_scale=plane,
-                        rhs=x_codes[g][:].bitcast(FP8X4),
-                        rhs_scale=x_plane[g][:],
-                        start=(g == 0 and half == 0),
-                        stop=(g == GROUPS - 1 and half == 1),
-                    )
+        def second(acc, codes, plane, g):
+            nc.tensor.matmul_mx(
+                out=acc[:], lhsT=codes.bitcast(FP8X4), lhsT_scale=plane,
+                rhs=x_codes[g][:].bitcast(FP8X4), rhs_scale=x_plane[g][:],
+                start=(g == 0), stop=(g == GROUPS - 1),
+            )
 
-        second_stage(0)
-        smaller(SLICES - 1)
-        quantize(x_codes[1], x_plane[1], weave(nc.vector.tensor_copy, 1))
-        second_stage(1)
+        def second_a(nb, g):
+            cols = slice(P * nb, P * (nb + 1))
+            second(ya_ps[nb], w3_codes[g][:, cols], w3_plane[g][:, cols], g)
 
-        tanh_sb = [keep.tile([P, 2, P3], F32, name="tanh_sb%d" % b) for b in range(2)]
-        sin_sb = [keep.tile([P, 2, P3], F32, name="sin_sb%d" % b) for b in range(2)]
-        for b in range(2):
-            nc.scalar.activation(tanh_sb[b][:], y_ps[b][:], ACT.Tanh)
-        for b in range(2):
-            nc.scalar.activation(sin_sb[b][:], y_ps[2 + b][:], ACT.Sin, scale=0.5)
-        for b in range(2):
-            sq = ring.tile([P, 2, P3], F32, name="sq")
-            nc.vector.scalar_tensor_tensor(sq[:], sin_sb[b][:], -2.0, sin_sb[b][:], ALU.mult, ALU.mult)
-            res = ring.tile([P, 2, P3], F32, name="res")
-            nc.vector.scalar_tensor_tensor(res[:], sq[:], 1.0, tanh_sb[b][:], ALU.add, ALU.mult)
-            nc.sync.dma_start(out[2 * P * b : 2 * P * (b + 1), :].rearrange("(h p) j -> p h j", p=P), res[:])
+        def second_b(nb, g):
+            cols = slice(P * nb, P * (nb + 1))
+            second(yb_ps[nb], w8_codes[:, g, cols], w8_plane[:, g, cols], g)
+
+        for nb in range(blocks):
+            second_a(nb, 0)
+            second_b(nb, 0)
+        quantize(x_codes[1][:], x_plane[1][:], weave(nc.vector.tensor_copy, 1)[:])
+
+        cos_less_one = {}
+
+        def sine(nb):
+            half = keep.tile([P, P3], F32, name="half%d" % nb)
+            nc.scalar.activation(half[:], yb_ps[nb][:], ACT.Sin, scale=0.5)
+            cos_less_one[nb] = keep.tile([P, P3], F32, name="cos_less_one%d" % nb)
+            nc.vector.scalar_tensor_tensor(cos_less_one[nb][:], half[:], -2.0, half[:], ALU.mult, ALU.mult)
+
+        def finish(nb):
+            th = keep.tile([P, P3], F32, name="th%d" % nb)
+            nc.scalar.activation(th[:], ya_ps[nb][:], ACT.Tanh)
+            res = keep.tile([P, P3], F32, name="res%d" % nb)
+            nc.vector.scalar_tensor_tensor(res[:], cos_less_one[nb][:], 1.0, th[:], ALU.add, ALU.mult)
+            nc.sync.dma_start(out[P * nb : P * (nb + 1), :], res[:])
+
+        for nb in range(blocks):
+            second_b(nb, 1)
+            sine(nb)
+        for nb in range(blocks):
+            second_a(nb, 1)
+            finish(nb)

@@ -25,8 +25,7 @@ CHUNK = 512
 CHUNKS = S // CHUNK
 QUADS = 4
 LIST_ROWS = 16
-OFFLOAD = [0, 1, 2, 2, 2, 2, 2, 2]
-G_WIDTH = 512
+OFFLOAD = [0, 0, 2, 2, 2, 2, 2, 2]
 
 
 def tile_list_pitch_jury_scores_kernel(
@@ -38,6 +37,7 @@ def tile_list_pitch_jury_scores_kernel(
         keep = ctx.enter_context(tc.tile_pool(name="keep", bufs=1))
         ring = ctx.enter_context(tc.tile_pool(name="ring", bufs=2))
         ring3 = ctx.enter_context(tc.tile_pool(name="ring3", bufs=3))
+        ring4 = ctx.enter_context(tc.tile_pool(name="ring4", bufs=4))
         psum = ctx.enter_context(tc.psum_pool(name="psum", bufs=4))
 
         def load_list(src, name):
@@ -130,11 +130,12 @@ def tile_list_pitch_jury_scores_kernel(
 
         ha_sb = {}
         hb_ps = {}
+        hb_sb = {}
         h_sb = {}
 
         def product_b(s, c):
             g, t = divmod(s, PACK)
-            hb_ps[s, c] = psum.tile([P, CHUNK], F32, name="bank_b")
+            hb_ps[s, c] = psum.tile([P, CHUNK], F32, name="bank_a" if c < OFFLOAD[s] else "bank_b")
             nc.tensor.matmul_mx(
                 out=hb_ps[s, c][:],
                 lhsT=w4_codes[g][:, 2 * P * t : 2 * P * (t + 1)].bitcast(FP4X4),
@@ -153,8 +154,7 @@ def tile_list_pitch_jury_scores_kernel(
             g, t = divmod(s, PACK)
             cols = slice(CHUNK * c, CHUNK * (c + 1))
             if c == 0:
-                ha_sb[s] = ring3.tile([P, S], F32, name="ha_sb")
-                h_sb[s] = ring.tile([P, S], F32, name="h_sb")
+                ha_sb[s] = ring4.tile([P, S], F32, name="ha_sb")
             ha_ps = psum.tile([P, CHUNK], F32, name="bank_a")
             nc.tensor.matmul_mx(
                 out=ha_ps[:],
@@ -166,23 +166,31 @@ def tile_list_pitch_jury_scores_kernel(
             )
             nc.scalar.copy(ha_sb[s][:, cols], ha_ps[:])
             if c < OFFLOAD[s]:
-                hb_sb = ring.tile([P, CHUNK], F32, name="hb_sb")
-                nc.scalar.copy(hb_sb[:], hb_ps[s, c][:])
-                for u in range(CHUNK // G_WIDTH):
-                    part = slice(G_WIDTH * u, G_WIDTH * (u + 1))
-                    whole = slice(CHUNK * c + G_WIDTH * u, CHUNK * c + G_WIDTH * (u + 1))
-                    excess = ring3.tile([P, G_WIDTH], F32, name="excess")
-                    nc.gpsimd.tensor_tensor(excess[:], hb_sb[:, part], ha_sb[s][:, whole], ALU.subtract)
-                    kept = ring3.tile([P, G_WIDTH], F32, name="kept")
-                    nc.scalar.activation(kept[:], excess[:], ACT.Relu)
-                    nc.gpsimd.tensor_tensor(h_sb[s][:, whole], ha_sb[s][:, whole], kept[:], ALU.add)
+                hb_sb[s, c] = ring.tile([P, CHUNK], F32, name="hb_sb")
+                nc.scalar.copy(hb_sb[s, c][:], hb_ps[s, c][:])
+
+        def new_h(s):
+            if s not in h_sb:
+                h_sb[s] = ring3.tile([P, S], F32, name="h_sb")
+            return h_sb[s]
+
+        def larger_off_vector(s, spare):
+            kept = {}
+            for c in range(OFFLOAD[s]):
+                cols = slice(CHUNK * c, CHUNK * (c + 1))
+                excess = spare[:, P1 * c : P1 * c + CHUNK]
+                nc.gpsimd.tensor_tensor(excess, hb_sb[s, c][:], ha_sb[s][:, cols], ALU.subtract)
+                kept[c] = ring.tile([P, CHUNK], F32, name="kept")
+                nc.scalar.activation(kept[c][:], excess, ACT.Relu)
+            for c in range(OFFLOAD[s]):
+                cols = slice(CHUNK * c, CHUNK * (c + 1))
+                nc.gpsimd.tensor_tensor(new_h(s)[:, cols], ha_sb[s][:, cols], kept[c][:], ALU.add)
 
         def larger(s, c):
-            if s >= SLICES or c < OFFLOAD[s]:
-                return
             cols = slice(CHUNK * c, CHUNK * (c + 1))
-            nc.vector.tensor_tensor(h_sb[s][:, cols], hb_ps[s, c][:], ha_sb[s][:, cols], ALU.max)
+            nc.vector.tensor_tensor(new_h(s)[:, cols], hb_ps[s, c][:], ha_sb[s][:, cols], ALU.max)
 
+        before = ring4.tile([P, S], F32, name="ha_sb")
         deal_w4_words(0)
         nc.vector.tensor_copy(v_plane[:], tab_plane[:].indirect(offs_sb[:]))
         deal_w4_plane(0)
@@ -212,6 +220,8 @@ def tile_list_pitch_jury_scores_kernel(
         larger(0, CHUNKS - 1)
         for c in range(CHUNKS):
             products(1, c)
+        for c in range(OFFLOAD[2]):
+            products(2, c)
         deal_w4_words(1)
         deal_w4_plane(1)
         w1_grouped = round_w1(1)
@@ -238,39 +248,47 @@ def tile_list_pitch_jury_scores_kernel(
         woven0 = None
         for k in range(SLICES + 2):
             level1, level2, level3 = k < SLICES, 1 <= k <= SLICES, k >= 2
-            spare = ha_sb[k] if level1 else ring3.tile([P, S], F32, name="ha_sb")
-            g4, g5, g6 = spare[:, 256:768], spare[:, 768:1024], spare[:, 0:256]
+            if k + 2 < SLICES:
+                larger_off_vector(k + 2, before)
+            if k + 3 < SLICES:
+                for c in range(OFFLOAD[k + 3]):
+                    products(k + 3, c)
+            spare = ha_sb[k] if level1 else ring4.tile([P, S], F32, name="ha_sb")
+            before = spare
+            g4, g5, g6 = spare[:, 1536:2048], spare[:, 1280:1536], spare[:, 0:256]
             if level1:
-                g2 = ring.tile([P, P1], F32, name="g2")
-                nc.vector.tensor_copy(g2[:], h_sb[k][:].indirect(p2_sb[:]))
+                g2 = spare[:, 256:1280]
+                nc.vector.tensor_copy(g2, h_sb[k][:].indirect(p2_sb[:]))
             if level2:
                 nc.vector.tensor_copy(g4, a1_sb[k - 1][:].indirect(p4_sb[:]))
             if level3:
                 nc.vector.tensor_copy(g5, a2_sb[k - 2][:].indirect(p5_sb[:]))
+                nc.vector.tensor_copy(g6, a2_sb[k - 2][:].indirect(p6_sb[:]))
+            if k + 1 < SLICES:
+                for c in range(OFFLOAD[k + 1], CHUNKS):
+                    larger(k + 1, c)
+            if k + 2 < SLICES:
+                for c in range(OFFLOAD[k + 2], CHUNKS):
+                    products(k + 2, c)
             if level1:
                 a1_sb[k] = ring.tile([P, P1], F32, name="a1")
-                nc.vector.tensor_tensor(a1_sb[k][:], h_sb[k][:].indirect(p1_sb[:]), g2[:], ALU.subtract)
-            if level3:
-                nc.vector.tensor_copy(g6, a2_sb[k - 2][:].indirect(p6_sb[:]))
+                nc.vector.tensor_tensor(a1_sb[k][:], h_sb[k][:].indirect(p1_sb[:]), g2, ALU.subtract)
+            if k == 0:
+                quantize(w1_codes[1][:], w1_plane[1][:], w1_grouped[:])
+            if k in (2, 3):
+                quantize(w3_codes[k - 2][:], w3_plane[k - 2][:], w3_grouped[k - 2][:])
+            if k == PACK + 2:
+                quantize(x_codes[0][:], x_plane[0][:], woven0[:])
             if level2:
                 a2_sb[k - 1] = ring.tile([P, P2], F32, name="a2")
                 nc.vector.tensor_tensor(a2_sb[k - 1][:], a1_sb[k - 1][:].indirect(p3_sb[:]), g4, ALU.mult)
             if level3:
                 pairs[k - 2] = (g5, g6)
                 smaller(k - 2)
-            for c in range(CHUNKS):
-                larger(k + 1, c)
-                products(k + 2, c)
-            if k == 0:
-                quantize(w1_codes[1][:], w1_plane[1][:], w1_grouped[:])
             if k in (1, 2):
                 w3_grouped[k - 1] = round_w3(w3_raw[k - 1])
-            if k in (2, 3):
-                quantize(w3_codes[k - 2][:], w3_plane[k - 2][:], w3_grouped[k - 2][:])
             if k == PACK + 1:
                 woven0 = weave(nc.scalar.copy, 0)
-            if k == PACK + 2:
-                quantize(x_codes[0][:], x_plane[0][:], woven0[:])
 
         blocks = N // P
         ya_ps = [psum.tile([P, P3], F32, name="bank_a") for nb in range(blocks)]

@@ -23,9 +23,14 @@ GROUPS = H // PASS
 SLICES = GROUPS * PACK
 CHUNK = 512
 CHUNKS = S // CHUNK
-QUADS = 4
+QUADRANT = 32
+SCALE_ROWS = 4
 LIST_ROWS = 16
-OFFLOAD = [0, 0, 2, 2, 2, 2, 2, 2]
+RUN = 4
+
+FIRST_SHARED = 3
+SHARED = 2
+SHARED_COLS = SHARED * CHUNK
 
 
 def tile_list_pitch_jury_scores_kernel(
@@ -36,9 +41,9 @@ def tile_list_pitch_jury_scores_kernel(
     with ExitStack() as ctx:
         keep = ctx.enter_context(tc.tile_pool(name="keep", bufs=1))
         ring = ctx.enter_context(tc.tile_pool(name="ring", bufs=2))
-        ring3 = ctx.enter_context(tc.tile_pool(name="ring3", bufs=3))
-        ring4 = ctx.enter_context(tc.tile_pool(name="ring4", bufs=4))
+        ring5 = ctx.enter_context(tc.tile_pool(name="ring5", bufs=5))
         psum = ctx.enter_context(tc.psum_pool(name="psum", bufs=4))
+
 
         def load_list(src, name):
             tile = keep.tile([P, src.shape[1]], U16, name=name)
@@ -49,13 +54,16 @@ def tile_list_pitch_jury_scores_kernel(
         w4_plane_raw = keep.tile([P, H], U8, align_bytes=64)
         w8_plane = keep.tile([P, GROUPS, N], U8, align_bytes=64)
         nc.gpsimd.memset(w8_plane[:].rearrange("p a n -> p (a n)").bitcast(I32), 0)
+        warm = keep.tile([P, 2], F32)
+        nc.gpsimd.memset(warm[:], 0.0)
+        nc.scalar.activation(warm[:, 1:2], warm[:, 0:1], ACT.Silu)
 
         def load_plane(plane, scales):
-            for q in range(QUADS):
-                rows = scales[0, 4 * q : 4 * q + 4, :].bitcast(I32)
+            for q in range(P // QUADRANT):
+                rows = scales[0, SCALE_ROWS * q : SCALE_ROWS * (q + 1), :].bitcast(I32)
                 nc.sync.dma_start(
-                    plane[32 * q : 32 * (q + 1), :].bitcast(I32),
-                    rows.unsqueeze(0).broadcast_to([8, 4, rows.shape[1]]),
+                    plane[QUADRANT * q : QUADRANT * (q + 1), :].bitcast(I32),
+                    rows.unsqueeze(0).broadcast_to([QUADRANT // SCALE_ROWS, SCALE_ROWS, rows.shape[1]]),
                 )
 
         def load_rows(src):
@@ -80,10 +88,10 @@ def tile_list_pitch_jury_scores_kernel(
         p6_sb = load_list(pos6, "p6_sb")
         w8_codes = keep.tile([P, GROUPS, N], I32, align_bytes=64)
         nc.sync.dma_start(w8_codes[:], w8_words.rearrange("a p n i -> p a (n i)").bitcast(I32))
-        for r in range(4):
+        for i in range(SCALE_ROWS):
             nc.sync.dma_start(
-                w8_plane[r:P:32, :, :].bitcast(I32),
-                w8_scales.rearrange("a (q r) n -> r q a n", r=4)[r].bitcast(I32),
+                w8_plane[i:P:QUADRANT, :, :].bitcast(I32),
+                w8_scales.rearrange("a (q i) n -> i q a n", i=SCALE_ROWS)[i].bitcast(I32),
             )
 
         w4_codes = [keep.tile([P, 2 * PASS], U8, align_bytes=64, name="w4_codes%d" % g) for g in range(GROUPS)]
@@ -92,50 +100,55 @@ def tile_list_pitch_jury_scores_kernel(
         w1_plane = [keep.tile([P, PASS], U8, align_bytes=64, name="w1_plane%d" % g) for g in range(GROUPS)]
         w3_codes = [keep.tile([P, N], U32, align_bytes=64, name="w3_codes%d" % g) for g in range(GROUPS)]
         w3_plane = [keep.tile([P, N], U8, align_bytes=64, name="w3_plane%d" % g) for g in range(GROUPS)]
-        x_codes = [keep.tile([P, P3], U32, align_bytes=64, name="x_codes%d" % g) for g in range(GROUPS)]
-        x_plane = [keep.tile([P, P3], U8, align_bytes=64, name="x_plane%d" % g) for g in range(GROUPS)]
+        a3_codes = [keep.tile([P, P3], U32, align_bytes=64, name="a3_codes%d" % g) for g in range(GROUPS)]
+        a3_plane = [keep.tile([P, P3], U8, align_bytes=64, name="a3_plane%d" % g) for g in range(GROUPS)]
         v_codes = {}
         v_plane = keep.tile([P, S], U8, align_bytes=64)
 
-        def deal_w4_words(g):
+
+        def order_w4_words(g):
             nc.gpsimd.tensor_copy(
                 w4_codes[g][:].rearrange("p (t m b) -> p t m b", t=PACK, b=2),
                 w4_raw[:, 2 * PASS * g : 2 * PASS * (g + 1)].rearrange("p (m t b) -> p t m b", t=PACK, b=2),
             )
 
-        def deal_w4_plane(g):
+        def order_w4_plane(g):
             nc.gpsimd.tensor_copy(
                 w4_plane[g][:].rearrange("p (t m) -> p t m", t=PACK),
                 w4_plane_raw[:, PASS * g : PASS * (g + 1)].rearrange("p (m t) -> p t m", t=PACK),
             )
 
         def round_w1(g):
-            grouped = ring.tile([P, PASS * PACK], BF16, align_bytes=64, name="grouped")
+            rounded = keep.tile([P, PASS * PACK], BF16, align_bytes=64, name="w1_rounded")
             nc.scalar.copy(
-                grouped[:].rearrange("p (t m j) -> p m j t", t=PACK, j=PACK),
+                rounded[:].rearrange("p (t m j) -> p m j t", t=PACK, j=PACK),
                 w1_raw[g][:].rearrange("p j (m t) -> p m j t", t=PACK),
             )
-            return grouped
+            return rounded
 
         def round_w3(raw):
-            grouped = ring.tile([P, N * PACK], BF16, align_bytes=64, name="grouped")
+            rounded = ring5.tile([P, N * PACK], BF16, align_bytes=64, name="ha_sb")
             nc.scalar.copy(
-                grouped[:].rearrange("p (c i j) -> p c j i", i=4, j=PACK),
-                raw[:].rearrange("p j (c i) -> p c j i", i=4),
+                rounded[:].rearrange("p (c i j) -> p c j i", i=RUN, j=PACK),
+                raw[:].rearrange("p j (c i) -> p c j i", i=RUN),
             )
-            return grouped
+            return rounded
 
-        def quantize(codes, plane, grouped):
-            nc.vector.quantize_mx(out=codes.bitcast(FP8X4), scales=plane, in_=grouped)
+        def quantize(codes, plane, rounded):
+            nc.vector.quantize_mx(out=codes.bitcast(FP8X4), scales=plane, in_=rounded)
+
 
         ha_sb = {}
         hb_ps = {}
         hb_sb = {}
         h_sb = {}
 
+        def shared_chunks(s):
+            return SHARED if FIRST_SHARED <= s < SLICES else 0
+
         def product_b(s, c):
             g, t = divmod(s, PACK)
-            hb_ps[s, c] = psum.tile([P, CHUNK], F32, name="bank_a" if c < OFFLOAD[s] else "bank_b")
+            hb_ps[s, c] = psum.tile([P, CHUNK], F32, name="bank_a" if c < shared_chunks(s) else "bank_b")
             nc.tensor.matmul_mx(
                 out=hb_ps[s, c][:],
                 lhsT=w4_codes[g][:, 2 * P * t : 2 * P * (t + 1)].bitcast(FP4X4),
@@ -145,16 +158,11 @@ def tile_list_pitch_jury_scores_kernel(
                 start=True, stop=True,
             )
 
-        def products(s, c):
-            if s < SLICES:
-                product_b(s, c)
-                product_a(s, c)
-
         def product_a(s, c):
             g, t = divmod(s, PACK)
             cols = slice(CHUNK * c, CHUNK * (c + 1))
             if c == 0:
-                ha_sb[s] = ring4.tile([P, S], F32, name="ha_sb")
+                ha_sb[s] = ring5.tile([P, S], F32, align_bytes=64, name="ha_sb")
             ha_ps = psum.tile([P, CHUNK], F32, name="bank_a")
             nc.tensor.matmul_mx(
                 out=ha_ps[:],
@@ -165,173 +173,168 @@ def tile_list_pitch_jury_scores_kernel(
                 start=True, stop=True,
             )
             nc.scalar.copy(ha_sb[s][:, cols], ha_ps[:])
-            if c < OFFLOAD[s]:
-                hb_sb[s, c] = ring.tile([P, CHUNK], F32, name="hb_sb")
-                nc.scalar.copy(hb_sb[s, c][:], hb_ps[s, c][:])
+            if c < shared_chunks(s):
+                if c == 0:
+                    hb_sb[s] = ring.tile([P, SHARED_COLS], F32, name="hb_sb")
+                nc.scalar.copy(hb_sb[s][:, cols], hb_ps[s, c][:])
 
-        def new_h(s):
+        def products(s, c):
+            product_b(s, c)
+            product_a(s, c)
+
+        def h_tile(s):
             if s not in h_sb:
-                h_sb[s] = ring3.tile([P, S], F32, name="h_sb")
+                h_sb[s] = ring.tile([P, S], F32, name="h_sb")
             return h_sb[s]
 
-        def larger_off_vector(s, spare):
-            kept = {}
-            for c in range(OFFLOAD[s]):
-                cols = slice(CHUNK * c, CHUNK * (c + 1))
-                excess = spare[:, P1 * c : P1 * c + CHUNK]
-                nc.gpsimd.tensor_tensor(excess, hb_sb[s, c][:], ha_sb[s][:, cols], ALU.subtract)
-                kept[c] = ring.tile([P, CHUNK], F32, name="kept")
-                nc.scalar.activation(kept[c][:], excess, ACT.Relu)
-            for c in range(OFFLOAD[s]):
-                cols = slice(CHUNK * c, CHUNK * (c + 1))
-                nc.gpsimd.tensor_tensor(new_h(s)[:, cols], ha_sb[s][:, cols], kept[c][:], ALU.add)
+        excess = {}
+
+        def excess_over_a(s, difference):
+            nc.gpsimd.tensor_tensor(difference, hb_sb[s][:], ha_sb[s][:, 0:SHARED_COLS], ALU.subtract)
+            excess[s] = ring.tile([P, SHARED_COLS], F32, name="excess")
+            nc.scalar.activation(excess[s][:], difference, ACT.Relu)
+
+        def add_excess(s):
+            nc.gpsimd.tensor_tensor(h_tile(s)[:, 0:SHARED_COLS], ha_sb[s][:, 0:SHARED_COLS], excess[s][:], ALU.add)
 
         def larger(s, c):
             cols = slice(CHUNK * c, CHUNK * (c + 1))
-            nc.vector.tensor_tensor(new_h(s)[:, cols], hb_ps[s, c][:], ha_sb[s][:, cols], ALU.max)
+            nc.vector.tensor_tensor(h_tile(s)[:, cols], hb_ps[s, c][:], ha_sb[s][:, cols], ALU.max)
 
-        before = ring4.tile([P, S], F32, name="ha_sb")
-        deal_w4_words(0)
+
+        last_chunk = CHUNKS - 1
+        for g in range(GROUPS):
+            order_w4_words(g)
         nc.vector.tensor_copy(v_plane[:], tab_plane[:].indirect(offs_sb[:]))
-        deal_w4_plane(0)
-        first = keep.tile([P, P * PACK], BF16, align_bytes=64, name="v_codes%d" % (CHUNKS - 1))
-        rest = keep.tile([P, (PACK - 1) * P * PACK], BF16, align_bytes=64)
-        by_slot = w1_raw[0][:].rearrange("p j (m t) -> p m j t", t=PACK)
-        nc.scalar.copy(first[:].rearrange("p (m j) -> p m j", j=PACK), by_slot[:, :, :, 0])
-        nc.gpsimd.tensor_copy(
-            rest[:].rearrange("p (t m j) -> p t m j", t=PACK - 1, j=PACK),
-            w1_raw[0][:].rearrange("p j (m t) -> p t m j", t=PACK)[:, 1:PACK, :, :],
-        )
-        per_chunk = CHUNK // LIST_ROWS
+        for g in range(GROUPS):
+            order_w4_plane(g)
+        w1_first = keep.tile([P, P * PACK], BF16, align_bytes=64, name="v_codes%d" % last_chunk)
+        w1_rest = keep.tile([P, (PACK - 1) * P * PACK], BF16, align_bytes=64)
+        by_slice = w1_raw[0][:].rearrange("p j (m t) -> p m j t", t=PACK)
+        nc.scalar.copy(w1_first[:].rearrange("p (m j) -> p m j", j=PACK), by_slice[:, :, :, 0])
+        for t in range(1, PACK):
+            nc.gpsimd.tensor_copy(
+                w1_rest[:, P * PACK * (t - 1) : P * PACK * t].rearrange("p (m j) -> p m j", j=PACK),
+                by_slice[:, :, :, t],
+            )
+        list_cols = CHUNK // LIST_ROWS
         for c in range(CHUNKS):
-            if c == CHUNKS - 1:
-                quantize(w1_codes[0][:, 0:P], w1_plane[0][:, 0:P], first[:])
-                for early in range(c):
-                    product_a(0, early)
+            if c == last_chunk:
+                quantize(w1_codes[0][:, 0:P], w1_plane[0][:, 0:P], w1_first[:])
+                for earlier in range(c):
+                    product_a(0, earlier)
             v_codes[c] = keep.tile([P, CHUNK], U32, align_bytes=64, name="v_codes%d" % c)
             nc.vector.tensor_copy(
-                v_codes[c][:], tab_sb[:].bitcast(U32).indirect(offs_sb[:, per_chunk * c : per_chunk * (c + 1)])
+                v_codes[c][:], tab_sb[:].bitcast(U32).indirect(offs_sb[:, list_cols * c : list_cols * (c + 1)])
             )
             product_b(0, c)
-        product_a(0, CHUNKS - 1)
-        for c in range(CHUNKS - 1):
+        product_a(0, last_chunk)
+        for c in range(last_chunk):
             larger(0, c)
-        quantize(w1_codes[0][:, P:PASS], w1_plane[0][:, P:PASS], rest[:])
-        larger(0, CHUNKS - 1)
+        quantize(w1_codes[0][:, P:PASS], w1_plane[0][:, P:PASS], w1_rest[:])
+        larger(0, last_chunk)
         for c in range(CHUNKS):
             products(1, c)
-        for c in range(OFFLOAD[2]):
-            products(2, c)
-        deal_w4_words(1)
-        deal_w4_plane(1)
-        w1_grouped = round_w1(1)
         w3_raw = [load_rows(w3[PASS * g : PASS * (g + 1), :]) for g in range(GROUPS)]
 
         a3_sb = [keep.tile([P, PACK, P3], BF16, name="a3_sb%d" % g) for g in range(GROUPS)]
-        pairs = {}
 
-        def smaller(s):
-            g, t = divmod(s, PACK)
-            nc.vector.tensor_tensor(a3_sb[g][:, t, :], pairs[s][0], pairs[s][1], ALU.min)
-
-        def weave(engine_copy, g):
+        def interleave_a3(engine_copy, g):
             woven = ring.tile([P, P3 * PACK], BF16, align_bytes=64, name="woven")
             engine_copy(
-                woven[:].rearrange("p (c i t) -> p c t i", i=4, t=PACK),
-                a3_sb[g][:].rearrange("p t (c i) -> p c t i", i=4),
+                woven[:].rearrange("p (c i t) -> p c t i", i=RUN, t=PACK),
+                a3_sb[g][:].rearrange("p t (c i) -> p c t i", i=RUN),
             )
             return woven
 
-        w3_grouped = {}
+
         a1_sb = {}
         a2_sb = {}
-        woven0 = None
+        w3_rounded = {}
+        h_p2 = {}
+        w3_round_period = SLICES - 2
+        group0_done_period = PACK + 1
         for k in range(SLICES + 2):
             level1, level2, level3 = k < SLICES, 1 <= k <= SLICES, k >= 2
-            if k + 2 < SLICES:
-                larger_off_vector(k + 2, before)
-            if k + 3 < SLICES:
-                for c in range(OFFLOAD[k + 3]):
-                    products(k + 3, c)
-            spare = ha_sb[k] if level1 else ring4.tile([P, S], F32, name="ha_sb")
-            before = spare
-            g4, g5, g6 = spare[:, 1536:2048], spare[:, 1280:1536], spare[:, 0:256]
+            if shared_chunks(k + 1):
+                add_excess(k + 1)
+            if shared_chunks(k + 2):
+                excess_over_a(k + 2, h_p2[k - 1])
+            spare = ha_sb[k] if level1 else ring5.tile([P, S], F32, align_bytes=64, name="ha_sb")
+            a2_p5, a2_p6, a1_p4 = spare[:, 0:P3], spare[:, P3 : 2 * P3], spare[:, P2 : 2 * P2]
             if level1:
-                g2 = spare[:, 256:1280]
-                nc.vector.tensor_copy(g2, h_sb[k][:].indirect(p2_sb[:]))
+                h_p2[k] = spare[:, P1 : 2 * P1]
+                nc.vector.tensor_copy(h_p2[k], h_sb[k][:].indirect(p2_sb[:]))
             if level2:
-                nc.vector.tensor_copy(g4, a1_sb[k - 1][:].indirect(p4_sb[:]))
+                nc.vector.tensor_copy(a1_p4, a1_sb[k - 1][:].indirect(p4_sb[:]))
             if level3:
-                nc.vector.tensor_copy(g5, a2_sb[k - 2][:].indirect(p5_sb[:]))
-                nc.vector.tensor_copy(g6, a2_sb[k - 2][:].indirect(p6_sb[:]))
+                nc.vector.tensor_copy(a2_p5, a2_sb[k - 2][:].indirect(p5_sb[:]))
+                nc.vector.tensor_copy(a2_p6, a2_sb[k - 2][:].indirect(p6_sb[:]))
             if k + 1 < SLICES:
-                for c in range(OFFLOAD[k + 1], CHUNKS):
+                for c in range(shared_chunks(k + 1), CHUNKS):
                     larger(k + 1, c)
             if k + 2 < SLICES:
-                for c in range(OFFLOAD[k + 2], CHUNKS):
+                for c in range(shared_chunks(k + 2), CHUNKS):
                     products(k + 2, c)
-            if level1:
-                a1_sb[k] = ring.tile([P, P1], F32, name="a1")
-                nc.vector.tensor_tensor(a1_sb[k][:], h_sb[k][:].indirect(p1_sb[:]), g2, ALU.subtract)
             if k == 0:
-                quantize(w1_codes[1][:], w1_plane[1][:], w1_grouped[:])
-            if k in (2, 3):
-                quantize(w3_codes[k - 2][:], w3_plane[k - 2][:], w3_grouped[k - 2][:])
-            if k == PACK + 2:
-                quantize(x_codes[0][:], x_plane[0][:], woven0[:])
+                w1_rounded = round_w1(1)
             if level2:
                 a2_sb[k - 1] = ring.tile([P, P2], F32, name="a2")
-                nc.vector.tensor_tensor(a2_sb[k - 1][:], a1_sb[k - 1][:].indirect(p3_sb[:]), g4, ALU.mult)
+                nc.vector.tensor_tensor(a2_sb[k - 1][:], a1_sb[k - 1][:].indirect(p3_sb[:]), a1_p4, ALU.mult)
+            if k == 1:
+                quantize(w1_codes[1][:], w1_plane[1][:], w1_rounded[:])
+            if k - w3_round_period - 1 in w3_rounded:
+                g = k - w3_round_period - 1
+                quantize(w3_codes[g][:], w3_plane[g][:], w3_rounded[g][:])
+            if k == group0_done_period + 1:
+                quantize(a3_codes[0][:], a3_plane[0][:], woven0[:])
             if level3:
-                pairs[k - 2] = (g5, g6)
-                smaller(k - 2)
-            if k in (1, 2):
-                w3_grouped[k - 1] = round_w3(w3_raw[k - 1])
-            if k == PACK + 1:
-                woven0 = weave(nc.scalar.copy, 0)
+                g, t = divmod(k - 2, PACK)
+                nc.vector.tensor_tensor(a3_sb[g][:, t, :], a2_p5, a2_p6, ALU.min)
+            if level1:
+                a1_sb[k] = ring.tile([P, P1], F32, name="a1")
+                nc.vector.tensor_tensor(a1_sb[k][:], h_sb[k][:].indirect(p1_sb[:]), h_p2[k], ALU.subtract)
+            for c in range(shared_chunks(k + 3)):
+                products(k + 3, c)
+            if 0 <= k - w3_round_period < GROUPS:
+                w3_rounded[k - w3_round_period] = round_w3(w3_raw[k - w3_round_period])
+            if k == group0_done_period:
+                woven0 = interleave_a3(nc.scalar.copy, 0)
+
 
         blocks = N // P
         ya_ps = [psum.tile([P, P3], F32, name="bank_a") for nb in range(blocks)]
         yb_ps = [psum.tile([P, P3], F32, name="bank_b") for nb in range(blocks)]
 
-        def second(acc, codes, plane, g):
+        def second_product(acc, codes, plane, g):
             nc.tensor.matmul_mx(
                 out=acc[:], lhsT=codes.bitcast(FP8X4), lhsT_scale=plane,
-                rhs=x_codes[g][:].bitcast(FP8X4), rhs_scale=x_plane[g][:],
+                rhs=a3_codes[g][:].bitcast(FP8X4), rhs_scale=a3_plane[g][:],
                 start=(g == 0), stop=(g == GROUPS - 1),
             )
 
-        def second_a(nb, g):
+        def pass_ya(nb, g):
             cols = slice(P * nb, P * (nb + 1))
-            second(ya_ps[nb], w3_codes[g][:, cols], w3_plane[g][:, cols], g)
+            second_product(ya_ps[nb], w3_codes[g][:, cols], w3_plane[g][:, cols], g)
 
-        def second_b(nb, g):
+        def pass_yb(nb, g):
             cols = slice(P * nb, P * (nb + 1))
-            second(yb_ps[nb], w8_codes[:, g, cols], w8_plane[:, g, cols], g)
+            second_product(yb_ps[nb], w8_codes[:, g, cols], w8_plane[:, g, cols], g)
 
         for nb in range(blocks):
-            second_a(nb, 0)
-            second_b(nb, 0)
-        quantize(x_codes[1][:], x_plane[1][:], weave(nc.vector.tensor_copy, 1)[:])
-
-        cos_less_one = {}
-
-        def sine(nb):
-            half = keep.tile([P, P3], F32, name="half%d" % nb)
-            nc.scalar.activation(half[:], yb_ps[nb][:], ACT.Sin, scale=0.5)
-            cos_less_one[nb] = keep.tile([P, P3], F32, name="cos_less_one%d" % nb)
-            nc.vector.scalar_tensor_tensor(cos_less_one[nb][:], half[:], -2.0, half[:], ALU.mult, ALU.mult)
-
-        def finish(nb):
-            th = keep.tile([P, P3], F32, name="th%d" % nb)
-            nc.scalar.activation(th[:], ya_ps[nb][:], ACT.Tanh)
-            res = keep.tile([P, P3], F32, name="res%d" % nb)
-            nc.vector.scalar_tensor_tensor(res[:], cos_less_one[nb][:], 1.0, th[:], ALU.add, ALU.mult)
-            nc.sync.dma_start(out[P * nb : P * (nb + 1), :], res[:])
+            pass_ya(nb, 0)
+            pass_yb(nb, 0)
+        quantize(a3_codes[1][:], a3_plane[1][:], interleave_a3(nc.vector.tensor_copy, 1)[:])
 
         for nb in range(blocks):
-            second_b(nb, 1)
-            sine(nb)
-        for nb in range(blocks):
-            second_a(nb, 1)
-            finish(nb)
+            pass_yb(nb, 1)
+            pass_ya(nb, 1)
+            sine = keep.tile([P, P3], F32, name="sine%d" % nb)
+            nc.scalar.activation(sine[:], yb_ps[nb][:], ACT.Sin, scale=0.5)
+            cos_less_one = keep.tile([P, P3], F32, name="cos_less_one%d" % nb)
+            nc.vector.scalar_tensor_tensor(cos_less_one[:], sine[:], -2.0, sine[:], ALU.mult, ALU.mult)
+            tanh_ya = keep.tile([P, P3], F32, name="tanh_ya%d" % nb)
+            nc.scalar.activation(tanh_ya[:], ya_ps[nb][:], ACT.Tanh)
+            score = keep.tile([P, P3], F32, name="score%d" % nb)
+            nc.vector.scalar_tensor_tensor(score[:], cos_less_one[:], 1.0, tanh_ya[:], ALU.add, ALU.mult)
+            nc.sync.dma_start(out[P * nb : P * (nb + 1), :], score[:])

from contextlib import ExitStack

import concourse.mybir as mybir

K, H, N, T, S, P1, P2, P3 = 512, 1024, 512, 4096, 2048, 1024, 512, 256
FLOPS = 2 * 2 * K * H * S + 2 * 2 * H * N * P3

F32 = mybir.dt.float32
BF16 = mybir.dt.bfloat16
I32 = mybir.dt.int32
U32 = mybir.dt.uint32
U16 = mybir.dt.uint16
U8 = mybir.dt.uint8
FP8X4 = mybir.dt.float8_e4m3fn_x4
FP4X4 = mybir.dt.float4_e2m1fn_x4
ALU = mybir.AluOpType
ACT = mybir.ActivationFunctionType

P = 128
PACK = 4
PASS = P * PACK
GROUPS = H // PASS
SLICES = GROUPS * PACK
CHUNK = 512
CHUNKS = S // CHUNK
QUADRANT = 32
SCALE_ROWS = 4
LIST_ROWS = 16
RUN = 4

FIRST_SHARED = 3
SHARED = 2
SHARED_COLS = SHARED * CHUNK


def tile_list_pitch_jury_scores_kernel(
    tc, tab_words, tab_scales, offs, pos1, pos2, pos3, pos4, pos5, pos6,
    w1, w4_words, w4_scales, w3, w8_words, w8_scales, out,
):
    nc = tc.nc
    with ExitStack() as ctx:
        keep = ctx.enter_context(tc.tile_pool(name="keep", bufs=1))
        ring = ctx.enter_context(tc.tile_pool(name="ring", bufs=2))
        ring5 = ctx.enter_context(tc.tile_pool(name="ring5", bufs=5))
        psum = ctx.enter_context(tc.psum_pool(name="psum", bufs=4))


        def load_list(src, name):
            tile = keep.tile([P, src.shape[1]], U16, name=name)
            nc.sync.dma_start(tile[:], src)
            return tile

        tab_plane = keep.tile([P, T], U8, align_bytes=64)
        w4_plane_raw = keep.tile([P, H], U8, align_bytes=64)
        w8_plane = keep.tile([P, GROUPS, N], U8, align_bytes=64)
        nc.gpsimd.memset(w8_plane[:].rearrange("p a n -> p (a n)").bitcast(I32), 0)
        warm = keep.tile([P, 2], F32)
        nc.gpsimd.memset(warm[:], 0.0)
        nc.scalar.activation(warm[:, 1:2], warm[:, 0:1], ACT.Silu)

        def load_plane(plane, scales):
            for q in range(P // QUADRANT):
                rows = scales[0, SCALE_ROWS * q : SCALE_ROWS * (q + 1), :].bitcast(I32)
                nc.sync.dma_start(
                    plane[QUADRANT * q : QUADRANT * (q + 1), :].bitcast(I32),
                    rows.unsqueeze(0).broadcast_to([QUADRANT // SCALE_ROWS, SCALE_ROWS, rows.shape[1]]),
                )

        def load_rows(src):
            raw = ring.tile([P, PACK, PASS], F32, name="raw")
            nc.sync.dma_start(raw[:], src.rearrange("(p j) c -> p j c", j=PACK))
            return raw

        offs_sb = load_list(offs, "offs_sb")
        load_plane(tab_plane, tab_scales)
        w4_raw = keep.tile([P, 2 * H], U8, align_bytes=64)
        nc.sync.dma_start(w4_raw[:].bitcast(I32), w4_words[0].bitcast(I32))
        tab_sb = keep.tile([P, T], I32, align_bytes=64)
        nc.sync.dma_start(tab_sb[:], tab_words[0].rearrange("p t i -> p (t i)").bitcast(I32))
        load_plane(w4_plane_raw, w4_scales)
        w1_raw = [load_rows(w1[:, 0:PASS])]
        p1_sb = load_list(pos1, "p1_sb")
        p2_sb = load_list(pos2, "p2_sb")
        w1_raw.append(load_rows(w1[:, PASS : 2 * PASS]))
        p3_sb = load_list(pos3, "p3_sb")
        p4_sb = load_list(pos4, "p4_sb")
        p5_sb = load_list(pos5, "p5_sb")
        p6_sb = load_list(pos6, "p6_sb")
        w8_codes = keep.tile([P, GROUPS, N], I32, align_bytes=64)
        nc.sync.dma_start(w8_codes[:], w8_words.rearrange("a p n i -> p a (n i)").bitcast(I32))
        for i in range(SCALE_ROWS):
            nc.sync.dma_start(
                w8_plane[i:P:QUADRANT, :, :].bitcast(I32),
                w8_scales.rearrange("a (q i) n -> i q a n", i=SCALE_ROWS)[i].bitcast(I32),
            )

        w4_codes = [keep.tile([P, 2 * PASS], U8, align_bytes=64, name="w4_codes%d" % g) for g in range(GROUPS)]
        w4_plane = [keep.tile([P, PASS], U8, align_bytes=64, name="w4_plane%d" % g) for g in range(GROUPS)]
        w1_codes = [keep.tile([P, PASS], U32, align_bytes=64, name="w1_codes%d" % g) for g in range(GROUPS)]
        w1_plane = [keep.tile([P, PASS], U8, align_bytes=64, name="w1_plane%d" % g) for g in range(GROUPS)]
        w3_codes = [keep.tile([P, N], U32, align_bytes=64, name="w3_codes%d" % g) for g in range(GROUPS)]
        w3_plane = [keep.tile([P, N], U8, align_bytes=64, name="w3_plane%d" % g) for g in range(GROUPS)]
        a3_codes = [keep.tile([P, P3], U32, align_bytes=64, name="a3_codes%d" % g) for g in range(GROUPS)]
        a3_plane = [keep.tile([P, P3], U8, align_bytes=64, name="a3_plane%d" % g) for g in range(GROUPS)]
        v_codes = {}
        v_plane = keep.tile([P, S], U8, align_bytes=64)


        def order_w4_words(g):
            nc.gpsimd.tensor_copy(
                w4_codes[g][:].rearrange("p (t m b) -> p t m b", t=PACK, b=2),
                w4_raw[:, 2 * PASS * g : 2 * PASS * (g + 1)].rearrange("p (m t b) -> p t m b", t=PACK, b=2),
            )

        def order_w4_plane(g):
            nc.gpsimd.tensor_copy(
                w4_plane[g][:].rearrange("p (t m) -> p t m", t=PACK),
                w4_plane_raw[:, PASS * g : PASS * (g + 1)].rearrange("p (m t) -> p t m", t=PACK),
            )

        def round_w1(g):
            rounded = keep.tile([P, PASS * PACK], BF16, align_bytes=64, name="w1_rounded")
            nc.scalar.copy(
                rounded[:].rearrange("p (t m j) -> p m j t", t=PACK, j=PACK),
                w1_raw[g][:].rearrange("p j (m t) -> p m j t", t=PACK),
            )
            return rounded

        def round_w3(raw):
            rounded = ring5.tile([P, N * PACK], BF16, align_bytes=64, name="ha_sb")
            nc.scalar.copy(
                rounded[:].rearrange("p (c i j) -> p c j i", i=RUN, j=PACK),
                raw[:].rearrange("p j (c i) -> p c j i", i=RUN),
            )
            return rounded

        def quantize(codes, plane, rounded):
            nc.vector.quantize_mx(out=codes.bitcast(FP8X4), scales=plane, in_=rounded)


        ha_sb = {}
        hb_ps = {}
        hb_sb = {}
        h_sb = {}

        def shared_chunks(s):
            return SHARED if FIRST_SHARED <= s < SLICES else 0

        def product_b(s, c):
            g, t = divmod(s, PACK)
            hb_ps[s, c] = psum.tile([P, CHUNK], F32, name="bank_a" if c < shared_chunks(s) else "bank_b")
            nc.tensor.matmul_mx(
                out=hb_ps[s, c][:],
                lhsT=w4_codes[g][:, 2 * P * t : 2 * P * (t + 1)].bitcast(FP4X4),
                lhsT_scale=w4_plane[g][:, P * t : P * (t + 1)],
                rhs=v_codes[c][:].bitcast(FP8X4),
                rhs_scale=v_plane[:, CHUNK * c : CHUNK * (c + 1)],
                start=True, stop=True,
            )

        def product_a(s, c):
            g, t = divmod(s, PACK)
            cols = slice(CHUNK * c, CHUNK * (c + 1))
            if c == 0:
                ha_sb[s] = ring5.tile([P, S], F32, align_bytes=64, name="ha_sb")
            ha_ps = psum.tile([P, CHUNK], F32, name="bank_a")
            nc.tensor.matmul_mx(
                out=ha_ps[:],
                lhsT=w1_codes[g][:, P * t : P * (t + 1)].bitcast(FP8X4),
                lhsT_scale=w1_plane[g][:, P * t : P * (t + 1)],
                rhs=v_codes[c][:].bitcast(FP8X4),
                rhs_scale=v_plane[:, cols],
                start=True, stop=True,
            )
            nc.scalar.copy(ha_sb[s][:, cols], ha_ps[:])
            if c < shared_chunks(s):
                if c == 0:
                    hb_sb[s] = ring.tile([P, SHARED_COLS], F32, name="hb_sb")
                nc.scalar.copy(hb_sb[s][:, cols], hb_ps[s, c][:])

        def products(s, c):
            product_b(s, c)
            product_a(s, c)

        def h_tile(s):
            if s not in h_sb:
                h_sb[s] = ring.tile([P, S], F32, name="h_sb")
            return h_sb[s]

        excess = {}

        def excess_over_a(s, difference):
            nc.gpsimd.tensor_tensor(difference, hb_sb[s][:], ha_sb[s][:, 0:SHARED_COLS], ALU.subtract)
            excess[s] = ring.tile([P, SHARED_COLS], F32, name="excess")
            nc.scalar.activation(excess[s][:], difference, ACT.Relu)

        def add_excess(s):
            nc.gpsimd.tensor_tensor(h_tile(s)[:, 0:SHARED_COLS], ha_sb[s][:, 0:SHARED_COLS], excess[s][:], ALU.add)

        def larger(s, c):
            cols = slice(CHUNK * c, CHUNK * (c + 1))
            nc.vector.tensor_tensor(h_tile(s)[:, cols], hb_ps[s, c][:], ha_sb[s][:, cols], ALU.max)


        last_chunk = CHUNKS - 1
        for g in range(GROUPS):
            order_w4_words(g)
        nc.vector.tensor_copy(v_plane[:], tab_plane[:].indirect(offs_sb[:]))
        for g in range(GROUPS):
            order_w4_plane(g)
        w1_first = keep.tile([P, P * PACK], BF16, align_bytes=64, name="v_codes%d" % last_chunk)
        w1_rest = keep.tile([P, (PACK - 1) * P * PACK], BF16, align_bytes=64)
        by_slice = w1_raw[0][:].rearrange("p j (m t) -> p m j t", t=PACK)
        nc.scalar.copy(w1_first[:].rearrange("p (m j) -> p m j", j=PACK), by_slice[:, :, :, 0])
        for t in range(1, PACK):
            nc.gpsimd.tensor_copy(
                w1_rest[:, P * PACK * (t - 1) : P * PACK * t].rearrange("p (m j) -> p m j", j=PACK),
                by_slice[:, :, :, t],
            )
        list_cols = CHUNK // LIST_ROWS
        for c in range(CHUNKS):
            if c == last_chunk:
                quantize(w1_codes[0][:, 0:P], w1_plane[0][:, 0:P], w1_first[:])
                for earlier in range(c):
                    product_a(0, earlier)
            v_codes[c] = keep.tile([P, CHUNK], U32, align_bytes=64, name="v_codes%d" % c)
            nc.vector.tensor_copy(
                v_codes[c][:], tab_sb[:].bitcast(U32).indirect(offs_sb[:, list_cols * c : list_cols * (c + 1)])
            )
            product_b(0, c)
        product_a(0, last_chunk)
        for c in range(last_chunk):
            larger(0, c)
        quantize(w1_codes[0][:, P:PASS], w1_plane[0][:, P:PASS], w1_rest[:])
        larger(0, last_chunk)
        for c in range(CHUNKS):
            products(1, c)
        w3_raw = [load_rows(w3[PASS * g : PASS * (g + 1), :]) for g in range(GROUPS)]

        a3_sb = [keep.tile([P, PACK, P3], BF16, name="a3_sb%d" % g) for g in range(GROUPS)]

        def interleave_a3(engine_copy, g):
            woven = ring.tile([P, P3 * PACK], BF16, align_bytes=64, name="woven")
            engine_copy(
                woven[:].rearrange("p (c i t) -> p c t i", i=RUN, t=PACK),
                a3_sb[g][:].rearrange("p t (c i) -> p c t i", i=RUN),
            )
            return woven


        a1_sb = {}
        a2_sb = {}
        w3_rounded = {}
        h_p2 = {}
        w3_round_period = SLICES - 2
        group0_done_period = PACK + 1
        for k in range(SLICES + 2):
            level1, level2, level3 = k < SLICES, 1 <= k <= SLICES, k >= 2
            if shared_chunks(k + 1):
                add_excess(k + 1)
            if shared_chunks(k + 2):
                excess_over_a(k + 2, h_p2[k - 1])
            spare = ha_sb[k] if level1 else ring5.tile([P, S], F32, align_bytes=64, name="ha_sb")
            a2_p5, a2_p6, a1_p4 = spare[:, 0:P3], spare[:, P3 : 2 * P3], spare[:, P2 : 2 * P2]
            if level1:
                h_p2[k] = spare[:, P1 : 2 * P1]
                nc.vector.tensor_copy(h_p2[k], h_sb[k][:].indirect(p2_sb[:]))
            if level2:
                nc.vector.tensor_copy(a1_p4, a1_sb[k - 1][:].indirect(p4_sb[:]))
            if level3:
                nc.vector.tensor_copy(a2_p5, a2_sb[k - 2][:].indirect(p5_sb[:]))
                nc.vector.tensor_copy(a2_p6, a2_sb[k - 2][:].indirect(p6_sb[:]))
            if k + 1 < SLICES:
                for c in range(shared_chunks(k + 1), CHUNKS):
                    larger(k + 1, c)
            if k + 2 < SLICES:
                for c in range(shared_chunks(k + 2), CHUNKS):
                    products(k + 2, c)
            if k == 0:
                w1_rounded = round_w1(1)
            if level2:
                a2_sb[k - 1] = ring.tile([P, P2], F32, name="a2")
                nc.vector.tensor_tensor(a2_sb[k - 1][:], a1_sb[k - 1][:].indirect(p3_sb[:]), a1_p4, ALU.mult)
            if k == 1:
                quantize(w1_codes[1][:], w1_plane[1][:], w1_rounded[:])
            if k - w3_round_period - 1 in w3_rounded:
                g = k - w3_round_period - 1
                quantize(w3_codes[g][:], w3_plane[g][:], w3_rounded[g][:])
            if k == group0_done_period + 1:
                quantize(a3_codes[0][:], a3_plane[0][:], woven0[:])
            if level3:
                g, t = divmod(k - 2, PACK)
                nc.vector.tensor_tensor(a3_sb[g][:, t, :], a2_p5, a2_p6, ALU.min)
            if level1:
                a1_sb[k] = ring.tile([P, P1], F32, name="a1")
                nc.vector.tensor_tensor(a1_sb[k][:], h_sb[k][:].indirect(p1_sb[:]), h_p2[k], ALU.subtract)
            for c in range(shared_chunks(k + 3)):
                products(k + 3, c)
            if 0 <= k - w3_round_period < GROUPS:
                w3_rounded[k - w3_round_period] = round_w3(w3_raw[k - w3_round_period])
            if k == group0_done_period:
                woven0 = interleave_a3(nc.scalar.copy, 0)


        blocks = N // P
        ya_ps = [psum.tile([P, P3], F32, name="bank_a") for nb in range(blocks)]
        yb_ps = [psum.tile([P, P3], F32, name="bank_b") for nb in range(blocks)]

        def second_product(acc, codes, plane, g):
            nc.tensor.matmul_mx(
                out=acc[:], lhsT=codes.bitcast(FP8X4), lhsT_scale=plane,
                rhs=a3_codes[g][:].bitcast(FP8X4), rhs_scale=a3_plane[g][:],
                start=(g == 0), stop=(g == GROUPS - 1),
            )

        def pass_ya(nb, g):
            cols = slice(P * nb, P * (nb + 1))
            second_product(ya_ps[nb], w3_codes[g][:, cols], w3_plane[g][:, cols], g)

        def pass_yb(nb, g):
            cols = slice(P * nb, P * (nb + 1))
            second_product(yb_ps[nb], w8_codes[:, g, cols], w8_plane[:, g, cols], g)

        for nb in range(blocks):
            pass_ya(nb, 0)
            pass_yb(nb, 0)
        quantize(a3_codes[1][:], a3_plane[1][:], interleave_a3(nc.vector.tensor_copy, 1)[:])

        for nb in range(blocks):
            pass_yb(nb, 1)
            pass_ya(nb, 1)
            sine = keep.tile([P, P3], F32, name="sine%d" % nb)
            nc.scalar.activation(sine[:], yb_ps[nb][:], ACT.Sin, scale=0.5)
            cos_less_one = keep.tile([P, P3], F32, name="cos_less_one%d" % nb)
            nc.vector.scalar_tensor_tensor(cos_less_one[:], sine[:], -2.0, sine[:], ALU.mult, ALU.mult)
            tanh_ya = keep.tile([P, P3], F32, name="tanh_ya%d" % nb)
            nc.scalar.activation(tanh_ya[:], ya_ps[nb][:], ACT.Tanh)
            score = keep.tile([P, P3], F32, name="score%d" % nb)
            nc.vector.scalar_tensor_tensor(score[:], cos_less_one[:], 1.0, tanh_ya[:], ALU.add, ALU.mult)
            nc.sync.dma_start(out[P * nb : P * (nb + 1), :], score[:])
